import numpy as np
import ml_dtypes


def mxq(x, axis, fmt="e4m3"):
    dtype, down = {"e4m3": (ml_dtypes.float8_e4m3fn, 7), "e5m2": (ml_dtypes.float8_e5m2, 14)}[fmt]
    v = np.moveaxis(np.asarray(x, np.float32).astype(ml_dtypes.bfloat16).astype(np.float64), axis, -1)
    blocks = v.reshape(v.shape[:-1] + (-1, 32))
    amax = np.abs(blocks).max(-1, keepdims=True)
    byte = np.maximum(np.where(amax > 0, np.frexp(amax)[1] - 1 + 127, 0) - down, 1)
    scale = np.exp2(byte - 127.0)
    codes = (blocks / scale).astype(np.float32).astype(dtype).astype(np.float64)
    return np.moveaxis((codes * scale).reshape(v.shape), -1, axis)


WIDE = False


def mx_kscale(k):
    if not WIDE:
        return np.ones(k)
    levels = np.array([10, -10, 5, -5, 0])
    if k % 512:
        return np.exp2(np.random.permutation(np.resize(levels, k // 32))).repeat(32)
    a = np.empty((k // 512, 16))
    for p in range(k // 512):
        a[p, :8] = np.random.permutation(np.resize(levels, 8))
        for g in range(8):
            far = levels[np.abs(levels - a[p, g]) >= 10]
            a[p, g + 8] = far[np.random.randint(len(far))]
    return np.exp2(a.ravel()).repeat(32)


def f64(x):
    return np.asarray(x).astype(np.float64)


def striped(idx):
    return np.tile(idx.reshape(-1, 16).T, (8, 1)).astype(np.uint16)


def unstriped(offs):
    return offs[:16].T.reshape(-1).astype(np.int64)


def silu(v):
    return v / (1.0 + np.exp(-np.maximum(v, -700.0)))


K, T, D, S, V, H, N = 1024, 2048, 2, 1024, 512, 512, 256


def setup_inputs():
    n = np.random.standard_normal
    s = mx_kscale(K)[:, None]
    u = mx_kscale(H)
    return {
        "xT": (n((K, T)) * s).astype(np.float32),
        "w1": (n((K, H)) / np.sqrt(K) / s * u).astype(np.float32),
        "w2": (n((H, N)) / np.sqrt(H) / u[:, None]).astype(np.float32),
        "gate": np.tile(np.random.uniform(0.5, 1.5, V), (N, 1)).astype(np.float32),
        "offs": striped(np.random.permutation(T)[:S]),
        "pos1": striped(np.random.permutation(2 * V)[:V]),
    }


def reference(xT, w1, w2, gate, offs, pos1):
    h = silu(mxq(f64(w1), 0, "e4m3").T @ mxq(f64(xT)[:, unstriped(offs)], 0, "e4m3"))
    z = h.reshape(H, V, D).max(axis=2)
    out = np.zeros((N, 2 * V))
    out[:, unstriped(pos1)] = f64(gate) * (mxq(f64(w2), 0, "e4m3").T @ mxq(z, 0, "e4m3"))
    return out

@@ -1,0 +1,216 @@
+from contextlib import ExitStack
+
+import concourse.mybir as mybir
+
+K, T, S, V, H, N = 1024, 2048, 1024, 512, 512, 256
+FLOPS = 2 * K * H * S + 2 * H * N * V
+
+F32 = mybir.dt.float32
+BF16 = mybir.dt.bfloat16
+I32 = mybir.dt.int32
+U32 = mybir.dt.uint32
+U16 = mybir.dt.uint16
+U8 = mybir.dt.uint8
+FP8X4 = mybir.dt.float8_e4m3fn_x4
+ACT = mybir.ActivationFunctionType
+ALU = mybir.AluOpType
+
+P = 128
+PACK = 4
+K_PASS = P * PACK
+PASSES = K // K_PASS
+ENTRIES = 256
+SLICES = S // ENTRIES
+POOLED = ENTRIES // 2
+BLOCKS = N // P
+
+CHUNKS = (
+    ((512, 256), (512, 256), (512, 256), (512, 256)),
+    ((512, 128), (512, 128), (512, 128), (256, 128), (256, 128)),
+)
+PLANE_ROW = (0, 4)
+STRETCHES = ((0, 256), (256, 256), (512, 512))
+
+
+def tile_picked_vpool_silu_e_kernel(tc, xT, w1, w2, gate, offs, pos1, out):
+    nc = tc.nc
+    with ExitStack() as ctx:
+        lists = ctx.enter_context(tc.tile_pool(name="lists", bufs=1))
+        keep = ctx.enter_context(tc.tile_pool(name="keep", bufs=1))
+        psum_h = ctx.enter_context(tc.psum_pool(name="psum_h", bufs=6))
+        psum_y = ctx.enter_context(tc.psum_pool(name="psum_y", bufs=2))
+
+        offs_t = lists.tile([P, S // 16], U16, name="offs_t")
+        pos_t = lists.tile([P, V // 16], U16, name="pos_t")
+
+        x_raw = []
+        for s in range(PASSES):
+            rows = xT[s * K_PASS : (s + 1) * K_PASS, :].rearrange("(p j) c -> p j c", j=PACK)
+            c0 = 0
+            for i, (n, nv) in enumerate(CHUNKS[s]):
+                raw = keep.tile([P, PACK, n], F32, name=f"x_raw{s}_{i}")
+                nc.sync.dma_start(out=raw[:], in_=rows[:, :, c0 : c0 + n])
+                x_raw.append((s, c0, n, nv, raw))
+                c0 += n
+                if s == 0 and i == 0:
+                    nc.sync.dma_start(offs_t[:], offs)
+        w1_raw = []
+        for s in range(PASSES):
+            raw = keep.tile([P, PACK, H], F32, name=f"w1_raw{s}")
+            nc.sync.dma_start(out=raw[:], in_=w1[s * K_PASS : (s + 1) * K_PASS, :].rearrange("(p j) c -> p j c", j=PACK))
+            w1_raw.append(raw)
+        w2_raw = keep.tile([P, PACK, N], F32, name="w2_raw")
+        nc.sync.dma_start(out=w2_raw[:], in_=w2.rearrange("(p j) c -> p j c", j=PACK))
+        nc.sync.dma_start(pos_t[:], pos1)
+        gate_sb = keep.tile([P, BLOCKS, V], F32, name="gate_sb")
+        nc.sync.dma_start(out=gate_sb[:], in_=gate.rearrange("(b p) v -> p b v", p=P))
+
+        warm_in = keep.tile([P, 2], F32, name="warm_in")
+        warm_out = keep.tile([P, 2], F32, name="warm_out")
+        nc.vector.memset(warm_in[:], 0.0)
+        nc.scalar.activation(warm_out[:], warm_in[:], ACT.Silu)
+        x_words = [keep.tile([P, T], U32, name=f"x_words{s}", align_bytes=64) for s in range(PASSES)]
+        x_bytes = keep.tile([P, T], U8, name="x_bytes", align_bytes=64)
+        nc.vector.memset(x_bytes[:].bitcast(I32), 0)
+        frames = [keep.tile([P, 2 * V], F32, name=f"frame{b}") for b in range(BLOCKS)]
+        for b in range(BLOCKS):
+            nc.gpsimd.memset(frames[b][:], 0.0)
+
+        def prepare_x(s, c0, n, nv, raw):
+            grouped = keep.tile([P, n, PACK], BF16, name=f"x_bf{s}_{c0}", align_bytes=64)
+            src = raw[:].rearrange("p j (c i) -> p c j i", i=4)
+            dst = grouped[:].rearrange("p (c i) j -> p c j i", i=4)
+            cut = (n - nv) // 4
+            nc.scalar.activation(dst[:, :cut], src[:, :cut], ACT.Copy)
+            nc.vector.tensor_copy(out=dst[:, cut:], in_=src[:, cut:])
+            nc.vector.quantize_mx(
+                out=x_words[s][:, c0 : c0 + n].bitcast(FP8X4),
+                scales=x_bytes[PLANE_ROW[s] :, c0 : c0 + n],
+                in_=grouped[:].rearrange("p c j -> p (c j)"),
+            )
+
+        picked_words = {}
+        picked_bytes = {}
+
+        def gather_words(s, e0, n, tag):
+            words = keep.tile([P, n], U32, name=f"g_words{s}_{e0}", tag=tag, align_bytes=64)
+            nc.vector.tensor_copy(out=words[:], in_=x_words[s][:].indirect(offs_t[:, e0 // 16 : (e0 + n) // 16]))
+            for e in range(e0, e0 + n, ENTRIES):
+                picked_words[s, e // ENTRIES] = words[:, e - e0 : e - e0 + ENTRIES].bitcast(FP8X4)
+
+        def gather_bytes(e0, n):
+            scale = keep.tile([P, n], U8, name=f"g_bytes{e0}", align_bytes=64)
+            nc.vector.tensor_copy(out=scale[:], in_=x_bytes[:].indirect(offs_t[:, e0 // 16 : (e0 + n) // 16]))
+            for e in range(e0, e0 + n, ENTRIES):
+                picked_bytes[e // ENTRIES] = scale[:, e - e0 : e - e0 + ENTRIES]
+
+        w1_codes = [keep.tile([P, H], U32, name=f"w1_codes{s}", align_bytes=64) for s in range(PASSES)]
+        w1_scales = [keep.tile([P, H], U8, name=f"w1_scales{s}", align_bytes=64) for s in range(PASSES)]
+
+        def prepare_w1(s, u, on_vector):
+            grouped = keep.tile([P, 2, P, PACK], BF16, name=f"w1_bf{s}_{u}", tag=f"w1_bf{s}_{u}", align_bytes=64)
+            src = w1_raw[s][:].rearrange("p j (m u e) -> p u m j e", u=2, e=2)[:, u]
+            dst = grouped[:].rearrange("p e m j -> p m j e")
+            cut = P - on_vector
+            nc.scalar.activation(dst[:, :cut], src[:, :cut], ACT.Copy)
+            if on_vector:
+                nc.vector.tensor_copy(out=dst[:, cut:], in_=src[:, cut:])
+            cols = slice(2 * P * u, 2 * P * (u + 1))
+            nc.vector.quantize_mx(
+                out=w1_codes[s][:, cols].bitcast(FP8X4),
+                scales=w1_scales[s][:, cols],
+                in_=grouped[:].rearrange("p e m j -> p (e m j)"),
+            )
+
+        for chunk in x_raw:
+            prepare_x(*chunk)
+        gather_words(0, 0, 512, "g_words0_0")
+        gather_words(0, 512, 512, "g_words0_1")
+        gather_bytes(*STRETCHES[0])
+        gather_words(1, *STRETCHES[0], "g_words1_0")
+        prepare_w1(0, 0, 0)
+        prepare_w1(0, 1, 0)
+        prepare_w1(1, 0, 72)
+        prepare_w1(1, 1, 0)
+        gather_bytes(*STRETCHES[1])
+        gather_words(1, *STRETCHES[1], "g_words1_1")
+        gather_bytes(*STRETCHES[2])
+        gather_words(1, *STRETCHES[2], "w1_bf1_1")
+
+        w2_codes = keep.tile([P, N], U32, name="w2_codes", align_bytes=64)
+        w2_scales = keep.tile([P, N], U8, name="w2_scales", align_bytes=64)
+        w2_bf = keep.tile([P, N, PACK], BF16, name="w2_bf", align_bytes=64)
+        nc.scalar.activation(
+            w2_bf[:].rearrange("p (c i) j -> p c j i", i=4),
+            w2_raw[:].rearrange("p j (c i) -> p c j i", i=4),
+            ACT.Copy,
+        )
+        nc.vector.quantize_mx(
+            out=w2_codes[:].bitcast(FP8X4), scales=w2_scales[:], in_=w2_bf[:].rearrange("p c j -> p (c j)")
+        )
+
+        y_sb = keep.tile([P, BLOCKS, V], F32, name="y_sb")
+
+        def first_layer(e0, n):
+            h = keep.tile([P, 2, n, 2], BF16, name=f"h{e0}", align_bytes=64)
+            for e1 in range(e0, e0 + n, ENTRIES):
+                q = e1 // ENTRIES
+                for u in range(2):
+                    bank = psum_h.tile([P, 2, ENTRIES], F32, name="h_bank")
+                    for e in range(2):
+                        cols = slice(P * (2 * u + e), P * (2 * u + e + 1))
+                        for s in range(PASSES):
+                            nc.tensor.matmul_mx(
+                                out=bank[:, e, :],
+                                lhsT=w1_codes[s][:, cols].bitcast(FP8X4),
+                                lhsT_scale=w1_scales[s][:, cols],
+                                rhs=picked_words[s, q],
+                                rhs_scale=picked_bytes[q][PLANE_ROW[s] :, :],
+                                start=(s == 0),
+                                stop=(s == PASSES - 1),
+                            )
+                    nc.scalar.activation(
+                        h[:, u, e1 - e0 : e1 - e0 + ENTRIES], bank[:].rearrange("p e j -> p j e"), ACT.Silu
+                    )
+            return h
+
+        def second_layer(e0, n, h):
+            v0, nv = e0 // 2, n // 2
+            z = keep.tile([P, nv, 2, 2], BF16, name=f"z{e0}", align_bytes=64)
+            pairs = h[:].rearrange("p u (v d) e -> p d v u e", d=2)
+            nc.vector.tensor_tensor(z[:], pairs[:, 0], pairs[:, 1], ALU.max)
+            z_codes = keep.tile([P, nv], U32, name=f"z_codes{e0}", align_bytes=64)
+            z_scales = keep.tile([P, nv], U8, name=f"z_scales{e0}", align_bytes=64)
+            nc.vector.quantize_mx(
+                out=z_codes[:].bitcast(FP8X4), scales=z_scales[:], in_=z[:].rearrange("p v u e -> p (v u e)")
+            )
+            bank = psum_y.tile([P, BLOCKS, nv], F32, name=f"y_bank{e0}", tag="y_bank")
+            for b in range(BLOCKS):
+                cols = slice(P * b, P * (b + 1))
+                nc.tensor.matmul_mx(
+                    out=bank[:, b, :],
+                    lhsT=w2_codes[:, cols].bitcast(FP8X4),
+                    lhsT_scale=w2_scales[:, cols],
+                    rhs=z_codes[:].bitcast(FP8X4),
+                    rhs_scale=z_scales[:],
+                    start=True,
+                    stop=True,
+                )
+            nc.scalar.activation(y_sb[:, :, v0 : v0 + nv], bank[:], ACT.Copy)
+
+        def scatter(b, e0, n):
+            v0, nv = e0 // 2, n // 2
+            cols = slice(v0, v0 + nv)
+            places = pos_t[:, v0 // 16 : (v0 + nv) // 16]
+            nc.vector.tensor_tensor(frames[b][:].indirect(places), y_sb[:, b, cols], gate_sb[:, b, cols], ALU.mult)
+
+        hs = [first_layer(*STRETCHES[0]), first_layer(*STRETCHES[1])]
+        second_layer(*STRETCHES[0], hs[0])
+        hs.append(first_layer(*STRETCHES[2]))
+        second_layer(*STRETCHES[1], hs[1])
+        second_layer(*STRETCHES[2], hs[2])
+        for stretch in STRETCHES:
+            for b in range(BLOCKS):
+                scatter(b, *stretch)
+                if stretch == STRETCHES[-1]:
+                    nc.sync.dma_start(out=out[P * b : P * (b + 1), :], in_=frames[b][:])

@@ -26,7 +26,7 @@ BLOCKS = N // P
 
 CHUNKS = (
     ((512, 256), (512, 256), (512, 256), (512, 256)),
-    ((512, 128), (512, 128), (512, 128), (256, 128), (256, 128)),
+    ((512, 96), (512, 96), (512, 96), (256, 64), (256, 128)),
 )
 PLANE_ROW = (0, 4)
 STRETCHES = ((0, 256), (256, 256), (512, 512))
@@ -56,7 +56,7 @@ def tile_picked_vpool_silu_e_kernel(tc, xT, w1, w2, gate, offs, pos1, out):
                     nc.sync.dma_start(offs_t[:], offs)
         w1_raw = []
         for s in range(PASSES):
-            raw = keep.tile([P, PACK, H], F32, name=f"w1_raw{s}")
+            raw = keep.tile([P, PACK, H], F32, name=f"w1_raw{s}", tag=f"w1_raw{s}", align_bytes=64)
             nc.sync.dma_start(out=raw[:], in_=w1[s * K_PASS : (s + 1) * K_PASS, :].rearrange("(p j) c -> p j c", j=PACK))
             w1_raw.append(raw)
         w2_raw = keep.tile([P, PACK, N], F32, name="w2_raw")
@@ -92,14 +92,16 @@ def tile_picked_vpool_silu_e_kernel(tc, xT, w1, w2, gate, offs, pos1, out):
         picked_words = {}
         picked_bytes = {}
 
-        def gather_words(s, e0, n, tag):
+        def gather_words(s, e0, n, tag, piece):
             words = keep.tile([P, n], U32, name=f"g_words{s}_{e0}", tag=tag, align_bytes=64)
-            nc.vector.tensor_copy(out=words[:], in_=x_words[s][:].indirect(offs_t[:, e0 // 16 : (e0 + n) // 16]))
+            for e in range(e0, e0 + n, piece):
+                entries = offs_t[:, e // 16 : (e + piece) // 16]
+                nc.vector.tensor_copy(out=words[:, e - e0 : e - e0 + piece], in_=x_words[s][:].indirect(entries))
             for e in range(e0, e0 + n, ENTRIES):
                 picked_words[s, e // ENTRIES] = words[:, e - e0 : e - e0 + ENTRIES].bitcast(FP8X4)
 
-        def gather_bytes(e0, n):
-            scale = keep.tile([P, n], U8, name=f"g_bytes{e0}", align_bytes=64)
+        def gather_bytes(e0, n, tag):
+            scale = keep.tile([P, n], U8, name=f"g_bytes{e0}", tag=tag, align_bytes=64)
             nc.vector.tensor_copy(out=scale[:], in_=x_bytes[:].indirect(offs_t[:, e0 // 16 : (e0 + n) // 16]))
             for e in range(e0, e0 + n, ENTRIES):
                 picked_bytes[e // ENTRIES] = scale[:, e - e0 : e - e0 + ENTRIES]
@@ -107,7 +109,9 @@ def tile_picked_vpool_silu_e_kernel(tc, xT, w1, w2, gate, offs, pos1, out):
         w1_codes = [keep.tile([P, H], U32, name=f"w1_codes{s}", align_bytes=64) for s in range(PASSES)]
         w1_scales = [keep.tile([P, H], U8, name=f"w1_scales{s}", align_bytes=64) for s in range(PASSES)]
 
-        def prepare_w1(s, u, on_vector):
+        w1_bf = {}
+
+        def round_w1(s, u, on_vector):
             grouped = keep.tile([P, 2, P, PACK], BF16, name=f"w1_bf{s}_{u}", tag=f"w1_bf{s}_{u}", align_bytes=64)
             src = w1_raw[s][:].rearrange("p j (m u e) -> p u m j e", u=2, e=2)[:, u]
             dst = grouped[:].rearrange("p e m j -> p m j e")
@@ -115,6 +119,10 @@ def tile_picked_vpool_silu_e_kernel(tc, xT, w1, w2, gate, offs, pos1, out):
             nc.scalar.activation(dst[:, :cut], src[:, :cut], ACT.Copy)
             if on_vector:
                 nc.vector.tensor_copy(out=dst[:, cut:], in_=src[:, cut:])
+            w1_bf[s, u] = grouped
+
+        def quantise_w1(s, u):
+            grouped = w1_bf[s, u]
             cols = slice(2 * P * u, 2 * P * (u + 1))
             nc.vector.quantize_mx(
                 out=w1_codes[s][:, cols].bitcast(FP8X4),
@@ -124,18 +132,34 @@ def tile_picked_vpool_silu_e_kernel(tc, xT, w1, w2, gate, offs, pos1, out):
 
         for chunk in x_raw:
             prepare_x(*chunk)
-        gather_words(0, 0, 512, "g_words0_0")
-        gather_words(0, 512, 512, "g_words0_1")
-        gather_bytes(*STRETCHES[0])
-        gather_words(1, *STRETCHES[0], "g_words1_0")
-        prepare_w1(0, 0, 0)
-        prepare_w1(0, 1, 0)
-        prepare_w1(1, 0, 72)
-        prepare_w1(1, 1, 0)
-        gather_bytes(*STRETCHES[1])
-        gather_words(1, *STRETCHES[1], "g_words1_1")
-        gather_bytes(*STRETCHES[2])
-        gather_words(1, *STRETCHES[2], "w1_bf1_1")
+        gather_words(0, 0, 512, "g_words0_0", 512)
+        gather_words(0, 512, 512, "g_words0_1", 512)
+        gather_bytes(*STRETCHES[0], "g_bytes0")
+        gather_words(1, *STRETCHES[0], "g_words1_0", ENTRIES)
+        round_w1(0, 0, 0)
+        quantise_w1(0, 0)
+        round_w1(0, 1, 0)
+        round_w1(1, 0, 72)
+        round_w1(1, 1, 32)
+        quantise_w1(1, 0)
+        quantise_w1(0, 1)
+        quantise_w1(1, 1)
+        gather_bytes(*STRETCHES[1], "g_bytes1")
+        gather_words(1, *STRETCHES[1], "g_words1_1", ENTRIES)
+        gather_bytes(512, 512, "w1_raw1")
+        gather_words(1, 512, 512, "w1_bf1_1", ENTRIES)
+
+        warm = psum_y.tile([P, BLOCKS, ENTRIES], F32, name="warm_bank", tag="y_bank")
+        for i in range(4):
+            nc.tensor.matmul_mx(
+                out=warm[:, i % 2, :],
+                lhsT=w1_codes[0][:, 0:P].bitcast(FP8X4),
+                lhsT_scale=w1_scales[0][:, 0:P],
+                rhs=picked_words[0, 0],
+                rhs_scale=picked_bytes[0],
+                start=True,
+                stop=True,
+            )
 
         w2_codes = keep.tile([P, N], U32, name="w2_codes", align_bytes=64)
         w2_scales = keep.tile([P, N], U8, name="w2_scales", align_bytes=64)
@@ -149,10 +173,10 @@ def tile_picked_vpool_silu_e_kernel(tc, xT, w1, w2, gate, offs, pos1, out):
             out=w2_codes[:].bitcast(FP8X4), scales=w2_scales[:], in_=w2_bf[:].rearrange("p c j -> p (c j)")
         )
 
-        y_sb = keep.tile([P, BLOCKS, V], F32, name="y_sb")
+        y_sb = {}
 
         def first_layer(e0, n):
-            h = keep.tile([P, 2, n, 2], BF16, name=f"h{e0}", align_bytes=64)
+            h = keep.tile([P, 2, n, 2], BF16, name=f"h{e0}", tag=f"h{e0}", align_bytes=64)
             for e1 in range(e0, e0 + n, ENTRIES):
                 q = e1 // ENTRIES
                 for u in range(2):
@@ -174,8 +198,8 @@ def tile_picked_vpool_silu_e_kernel(tc, xT, w1, w2, gate, offs, pos1, out):
                     )
             return h
 
-        def second_layer(e0, n, h):
-            v0, nv = e0 // 2, n // 2
+        def pool_and_quantise(e0, n, h):
+            nv = n // 2
             z = keep.tile([P, nv, 2, 2], BF16, name=f"z{e0}", align_bytes=64)
             pairs = h[:].rearrange("p u (v d) e -> p d v u e", d=2)
             nc.vector.tensor_tensor(z[:], pairs[:, 0], pairs[:, 1], ALU.max)
@@ -184,6 +208,10 @@ def tile_picked_vpool_silu_e_kernel(tc, xT, w1, w2, gate, offs, pos1, out):
             nc.vector.quantize_mx(
                 out=z_codes[:].bitcast(FP8X4), scales=z_scales[:], in_=z[:].rearrange("p v u e -> p (v u e)")
             )
+            return z_codes, z_scales
+
+        def second_layer(e0, n, z_codes, z_scales, tag):
+            nv = n // 2
             bank = psum_y.tile([P, BLOCKS, nv], F32, name=f"y_bank{e0}", tag="y_bank")
             for b in range(BLOCKS):
                 cols = slice(P * b, P * (b + 1))
@@ -196,19 +224,22 @@ def tile_picked_vpool_silu_e_kernel(tc, xT, w1, w2, gate, offs, pos1, out):
                     start=True,
                     stop=True,
                 )
-            nc.scalar.activation(y_sb[:, :, v0 : v0 + nv], bank[:], ACT.Copy)
+            y_sb[e0] = keep.tile([P, BLOCKS, nv], F32, name=f"y{e0}", tag=tag, align_bytes=64)
+            nc.scalar.activation(y_sb[e0][:], bank[:], ACT.Copy)
 
         def scatter(b, e0, n):
             v0, nv = e0 // 2, n // 2
             cols = slice(v0, v0 + nv)
             places = pos_t[:, v0 // 16 : (v0 + nv) // 16]
-            nc.vector.tensor_tensor(frames[b][:].indirect(places), y_sb[:, b, cols], gate_sb[:, b, cols], ALU.mult)
+            nc.vector.tensor_tensor(frames[b][:].indirect(places), y_sb[e0][:, b, :], gate_sb[:, b, cols], ALU.mult)
 
         hs = [first_layer(*STRETCHES[0]), first_layer(*STRETCHES[1])]
-        second_layer(*STRETCHES[0], hs[0])
+        second_layer(*STRETCHES[0], *pool_and_quantise(*STRETCHES[0], hs[0]), "y0")
         hs.append(first_layer(*STRETCHES[2]))
-        second_layer(*STRETCHES[1], hs[1])
-        second_layer(*STRETCHES[2], hs[2])
+        z1 = pool_and_quantise(*STRETCHES[1], hs[1])
+        z2 = pool_and_quantise(*STRETCHES[2], hs[2])
+        second_layer(*STRETCHES[1], *z1, "h512")
+        second_layer(*STRETCHES[2], *z2, "y2")
         for stretch in STRETCHES:
             for b in range(BLOCKS):
                 scatter(b, *stretch)

@@ -28,6 +28,7 @@ CHUNKS = (
     ((512, 256), (512, 256), (512, 256), (512, 256)),
     ((512, 96), (512, 96), (512, 96), (256, 64), (256, 128)),
 )
+LOADS = ((1024, 1024), (512, 512, 512, 256, 256))
 PLANE_ROW = (0, 4)
 STRETCHES = ((0, 256), (256, 256), (512, 512))
 
@@ -46,14 +47,21 @@ def tile_picked_vpool_silu_e_kernel(tc, xT, w1, w2, gate, offs, pos1, out):
         x_raw = []
         for s in range(PASSES):
             rows = xT[s * K_PASS : (s + 1) * K_PASS, :].rearrange("(p j) c -> p j c", j=PACK)
+            loaded = []
             c0 = 0
-            for i, (n, nv) in enumerate(CHUNKS[s]):
-                raw = keep.tile([P, PACK, n], F32, name=f"x_raw{s}_{i}")
+            for n in LOADS[s]:
+                raw = keep.tile([P, PACK, n], F32, name=f"x_raw{s}_{c0}")
                 nc.sync.dma_start(out=raw[:], in_=rows[:, :, c0 : c0 + n])
-                x_raw.append((s, c0, n, nv, raw))
-                c0 += n
-                if s == 0 and i == 0:
+                loaded.append((c0, n, raw))
+                if s == 0 and c0 == 0:
                     nc.sync.dma_start(offs_t[:], offs)
+                c0 += n
+            c0 = 0
+            for n, nv in CHUNKS[s]:
+                for r0, rn, raw in loaded:
+                    if r0 <= c0 < r0 + rn:
+                        x_raw.append((s, c0, n, nv, raw[:, :, c0 - r0 : c0 - r0 + n]))
+                c0 += n
         w1_raw = []
         for s in range(PASSES):
             raw = keep.tile([P, PACK, H], F32, name=f"w1_raw{s}", tag=f"w1_raw{s}", align_bytes=64)
@@ -78,7 +86,7 @@ def tile_picked_vpool_silu_e_kernel(tc, xT, w1, w2, gate, offs, pos1, out):
 
         def prepare_x(s, c0, n, nv, raw):
             grouped = keep.tile([P, n, PACK], BF16, name=f"x_bf{s}_{c0}", align_bytes=64)
-            src = raw[:].rearrange("p j (c i) -> p c j i", i=4)
+            src = raw.rearrange("p j (c i) -> p c j i", i=4)
             dst = grouped[:].rearrange("p (c i) j -> p c j i", i=4)
             cut = (n - nv) // 4
             nc.scalar.activation(dst[:, :cut], src[:, :cut], ACT.Copy)
@@ -134,20 +142,19 @@ def tile_picked_vpool_silu_e_kernel(tc, xT, w1, w2, gate, offs, pos1, out):
             prepare_x(*chunk)
         gather_words(0, 0, 512, "g_words0_0", 512)
         gather_words(0, 512, 512, "g_words0_1", 512)
-        gather_bytes(*STRETCHES[0], "g_bytes0")
-        gather_words(1, *STRETCHES[0], "g_words1_0", ENTRIES)
+        gather_bytes(0, 512, "g_bytes0")
+        gather_words(1, 0, 512, "g_words1_0", 512)
         round_w1(0, 0, 0)
         quantise_w1(0, 0)
         round_w1(0, 1, 0)
-        round_w1(1, 0, 72)
-        round_w1(1, 1, 32)
+        round_w1(1, 0, 64)
+        round_w1(1, 1, 64)
         quantise_w1(1, 0)
         quantise_w1(0, 1)
         quantise_w1(1, 1)
-        gather_bytes(*STRETCHES[1], "g_bytes1")
-        gather_words(1, *STRETCHES[1], "g_words1_1", ENTRIES)
-        gather_bytes(512, 512, "w1_raw1")
-        gather_words(1, 512, 512, "w1_bf1_1", ENTRIES)
+        gather_bytes(512, 256, "w1_bf0_0")
+        gather_words(1, 512, 256, "w1_bf1_1", ENTRIES)
+        gather_bytes(768, 256, "w1_raw1")
 
         warm = psum_y.tile([P, BLOCKS, ENTRIES], F32, name="warm_bank", tag="y_bank")
         for i in range(4):
@@ -200,7 +207,7 @@ def tile_picked_vpool_silu_e_kernel(tc, xT, w1, w2, gate, offs, pos1, out):
 
         def pool_and_quantise(e0, n, h):
             nv = n // 2
-            z = keep.tile([P, nv, 2, 2], BF16, name=f"z{e0}", align_bytes=64)
+            z = keep.tile([P, nv, 2, 2], BF16, name=f"z{e0}", tag=f"z{e0}", align_bytes=64)
             pairs = h[:].rearrange("p u (v d) e -> p d v u e", d=2)
             nc.vector.tensor_tensor(z[:], pairs[:, 0], pairs[:, 1], ALU.max)
             z_codes = keep.tile([P, nv], U32, name=f"z_codes{e0}", align_bytes=64)
@@ -235,6 +242,7 @@ def tile_picked_vpool_silu_e_kernel(tc, xT, w1, w2, gate, offs, pos1, out):
 
         hs = [first_layer(*STRETCHES[0]), first_layer(*STRETCHES[1])]
         second_layer(*STRETCHES[0], *pool_and_quantise(*STRETCHES[0], hs[0]), "y0")
+        gather_words(1, 768, 256, "z0", ENTRIES)
         hs.append(first_layer(*STRETCHES[2]))
         z1 = pool_and_quantise(*STRETCHES[1], hs[1])
         z2 = pool_and_quantise(*STRETCHES[2], hs[2])

from contextlib import ExitStack

import concourse.mybir as mybir

K, T, S, V, H, N = 1024, 2048, 1024, 512, 512, 256
FLOPS = 2 * K * H * S + 2 * H * N * V

F32 = mybir.dt.float32
BF16 = mybir.dt.bfloat16
I32 = mybir.dt.int32
U32 = mybir.dt.uint32
U16 = mybir.dt.uint16
U8 = mybir.dt.uint8
FP8X4 = mybir.dt.float8_e4m3fn_x4
ACT = mybir.ActivationFunctionType
ALU = mybir.AluOpType

P = 128
PACK = 4
K_PASS = P * PACK
PASSES = K // K_PASS
ENTRIES = 256
SLICES = S // ENTRIES
POOLED = ENTRIES // 2
BLOCKS = N // P

CHUNKS = (
    ((512, 256), (512, 256), (512, 256), (512, 256)),
    ((512, 96), (512, 96), (512, 96), (256, 64), (256, 128)),
)
LOADS = ((1024, 1024), (512, 512, 512, 256, 256))
PLANE_ROW = (0, 4)
STRETCHES = ((0, 256), (256, 256), (512, 512))


def tile_picked_vpool_silu_e_kernel(tc, xT, w1, w2, gate, offs, pos1, out):
    nc = tc.nc
    with ExitStack() as ctx:
        lists = ctx.enter_context(tc.tile_pool(name="lists", bufs=1))
        keep = ctx.enter_context(tc.tile_pool(name="keep", bufs=1))
        psum_h = ctx.enter_context(tc.psum_pool(name="psum_h", bufs=6))
        psum_y = ctx.enter_context(tc.psum_pool(name="psum_y", bufs=2))

        offs_t = lists.tile([P, S // 16], U16, name="offs_t")
        pos_t = lists.tile([P, V // 16], U16, name="pos_t")

        x_raw = []
        for s in range(PASSES):
            rows = xT[s * K_PASS : (s + 1) * K_PASS, :].rearrange("(p j) c -> p j c", j=PACK)
            loaded = []
            c0 = 0
            for n in LOADS[s]:
                raw = keep.tile([P, PACK, n], F32, name=f"x_raw{s}_{c0}")
                nc.sync.dma_start(out=raw[:], in_=rows[:, :, c0 : c0 + n])
                loaded.append((c0, n, raw))
                if s == 0 and c0 == 0:
                    nc.sync.dma_start(offs_t[:], offs)
                c0 += n
            c0 = 0
            for n, nv in CHUNKS[s]:
                for r0, rn, raw in loaded:
                    if r0 <= c0 < r0 + rn:
                        x_raw.append((s, c0, n, nv, raw[:, :, c0 - r0 : c0 - r0 + n]))
                c0 += n
        w1_raw = []
        for s in range(PASSES):
            raw = keep.tile([P, PACK, H], F32, name=f"w1_raw{s}", tag=f"w1_raw{s}", align_bytes=64)
            nc.sync.dma_start(out=raw[:], in_=w1[s * K_PASS : (s + 1) * K_PASS, :].rearrange("(p j) c -> p j c", j=PACK))
            w1_raw.append(raw)
        w2_raw = keep.tile([P, PACK, N], F32, name="w2_raw")
        nc.sync.dma_start(out=w2_raw[:], in_=w2.rearrange("(p j) c -> p j c", j=PACK))
        nc.sync.dma_start(pos_t[:], pos1)
        gate_sb = keep.tile([P, BLOCKS, V], F32, name="gate_sb")
        nc.sync.dma_start(out=gate_sb[:], in_=gate.rearrange("(b p) v -> p b v", p=P))

        warm_in = keep.tile([P, 2], F32, name="warm_in")
        warm_out = keep.tile([P, 2], F32, name="warm_out")
        nc.vector.memset(warm_in[:], 0.0)
        nc.scalar.activation(warm_out[:], warm_in[:], ACT.Silu)
        x_words = [keep.tile([P, T], U32, name=f"x_words{s}", align_bytes=64) for s in range(PASSES)]
        x_bytes = keep.tile([P, T], U8, name="x_bytes", align_bytes=64)
        nc.vector.memset(x_bytes[:].bitcast(I32), 0)
        frames = [keep.tile([P, 2 * V], F32, name=f"frame{b}") for b in range(BLOCKS)]
        for b in range(BLOCKS):
            nc.gpsimd.memset(frames[b][:], 0.0)

        def prepare_x(s, c0, n, nv, raw):
            grouped = keep.tile([P, n, PACK], BF16, name=f"x_bf{s}_{c0}", align_bytes=64)
            src = raw.rearrange("p j (c i) -> p c j i", i=4)
            dst = grouped[:].rearrange("p (c i) j -> p c j i", i=4)
            cut = (n - nv) // 4
            nc.scalar.activation(dst[:, :cut], src[:, :cut], ACT.Copy)
            nc.vector.tensor_copy(out=dst[:, cut:], in_=src[:, cut:])
            nc.vector.quantize_mx(
                out=x_words[s][:, c0 : c0 + n].bitcast(FP8X4),
                scales=x_bytes[PLANE_ROW[s] :, c0 : c0 + n],
                in_=grouped[:].rearrange("p c j -> p (c j)"),
            )

        picked_words = {}
        picked_bytes = {}

        def gather_words(s, e0, n, tag, piece):
            words = keep.tile([P, n], U32, name=f"g_words{s}_{e0}", tag=tag, align_bytes=64)
            for e in range(e0, e0 + n, piece):
                entries = offs_t[:, e // 16 : (e + piece) // 16]
                nc.vector.tensor_copy(out=words[:, e - e0 : e - e0 + piece], in_=x_words[s][:].indirect(entries))
            for e in range(e0, e0 + n, ENTRIES):
                picked_words[s, e // ENTRIES] = words[:, e - e0 : e - e0 + ENTRIES].bitcast(FP8X4)

        def gather_bytes(e0, n, tag):
            scale = keep.tile([P, n], U8, name=f"g_bytes{e0}", tag=tag, align_bytes=64)
            nc.vector.tensor_copy(out=scale[:], in_=x_bytes[:].indirect(offs_t[:, e0 // 16 : (e0 + n) // 16]))
            for e in range(e0, e0 + n, ENTRIES):
                picked_bytes[e // ENTRIES] = scale[:, e - e0 : e - e0 + ENTRIES]

        w1_codes = [keep.tile([P, H], U32, name=f"w1_codes{s}", align_bytes=64) for s in range(PASSES)]
        w1_scales = [keep.tile([P, H], U8, name=f"w1_scales{s}", align_bytes=64) for s in range(PASSES)]

        w1_bf = {}

        def round_w1(s, u, on_vector):
            grouped = keep.tile([P, 2, P, PACK], BF16, name=f"w1_bf{s}_{u}", tag=f"w1_bf{s}_{u}", align_bytes=64)
            src = w1_raw[s][:].rearrange("p j (m u e) -> p u m j e", u=2, e=2)[:, u]
            dst = grouped[:].rearrange("p e m j -> p m j e")
            cut = P - on_vector
            nc.scalar.activation(dst[:, :cut], src[:, :cut], ACT.Copy)
            if on_vector:
                nc.vector.tensor_copy(out=dst[:, cut:], in_=src[:, cut:])
            w1_bf[s, u] = grouped

        def quantise_w1(s, u):
            grouped = w1_bf[s, u]
            cols = slice(2 * P * u, 2 * P * (u + 1))
            nc.vector.quantize_mx(
                out=w1_codes[s][:, cols].bitcast(FP8X4),
                scales=w1_scales[s][:, cols],
                in_=grouped[:].rearrange("p e m j -> p (e m j)"),
            )

        for chunk in x_raw:
            prepare_x(*chunk)
        gather_words(0, 0, 512, "g_words0_0", 512)
        gather_words(0, 512, 512, "g_words0_1", 512)
        gather_bytes(0, 512, "g_bytes0")
        gather_words(1, 0, 512, "g_words1_0", 512)
        round_w1(0, 0, 0)
        quantise_w1(0, 0)
        round_w1(0, 1, 0)
        round_w1(1, 0, 64)
        round_w1(1, 1, 64)
        quantise_w1(1, 0)
        quantise_w1(0, 1)
        quantise_w1(1, 1)
        gather_bytes(512, 256, "w1_bf0_0")
        gather_words(1, 512, 256, "w1_bf1_1", ENTRIES)
        gather_bytes(768, 256, "w1_raw1")

        warm = psum_y.tile([P, BLOCKS, ENTRIES], F32, name="warm_bank", tag="y_bank")
        for i in range(4):
            nc.tensor.matmul_mx(
                out=warm[:, i % 2, :],
                lhsT=w1_codes[0][:, 0:P].bitcast(FP8X4),
                lhsT_scale=w1_scales[0][:, 0:P],
                rhs=picked_words[0, 0],
                rhs_scale=picked_bytes[0],
                start=True,
                stop=True,
            )

        w2_codes = keep.tile([P, N], U32, name="w2_codes", align_bytes=64)
        w2_scales = keep.tile([P, N], U8, name="w2_scales", align_bytes=64)
        w2_bf = keep.tile([P, N, PACK], BF16, name="w2_bf", align_bytes=64)
        nc.scalar.activation(
            w2_bf[:].rearrange("p (c i) j -> p c j i", i=4),
            w2_raw[:].rearrange("p j (c i) -> p c j i", i=4),
            ACT.Copy,
        )
        nc.vector.quantize_mx(
            out=w2_codes[:].bitcast(FP8X4), scales=w2_scales[:], in_=w2_bf[:].rearrange("p c j -> p (c j)")
        )

        y_sb = {}

        def first_layer(e0, n):
            h = keep.tile([P, 2, n, 2], BF16, name=f"h{e0}", tag=f"h{e0}", align_bytes=64)
            for e1 in range(e0, e0 + n, ENTRIES):
                q = e1 // ENTRIES
                for u in range(2):
                    bank = psum_h.tile([P, 2, ENTRIES], F32, name="h_bank")
                    for e in range(2):
                        cols = slice(P * (2 * u + e), P * (2 * u + e + 1))
                        for s in range(PASSES):
                            nc.tensor.matmul_mx(
                                out=bank[:, e, :],
                                lhsT=w1_codes[s][:, cols].bitcast(FP8X4),
                                lhsT_scale=w1_scales[s][:, cols],
                                rhs=picked_words[s, q],
                                rhs_scale=picked_bytes[q][PLANE_ROW[s] :, :],
                                start=(s == 0),
                                stop=(s == PASSES - 1),
                            )
                    nc.scalar.activation(
                        h[:, u, e1 - e0 : e1 - e0 + ENTRIES], bank[:].rearrange("p e j -> p j e"), ACT.Silu
                    )
            return h

        def pool_and_quantise(e0, n, h):
            nv = n // 2
            z = keep.tile([P, nv, 2, 2], BF16, name=f"z{e0}", tag=f"z{e0}", align_bytes=64)
            pairs = h[:].rearrange("p u (v d) e -> p d v u e", d=2)
            nc.vector.tensor_tensor(z[:], pairs[:, 0], pairs[:, 1], ALU.max)
            z_codes = keep.tile([P, nv], U32, name=f"z_codes{e0}", align_bytes=64)
            z_scales = keep.tile([P, nv], U8, name=f"z_scales{e0}", align_bytes=64)
            nc.vector.quantize_mx(
                out=z_codes[:].bitcast(FP8X4), scales=z_scales[:], in_=z[:].rearrange("p v u e -> p (v u e)")
            )
            return z_codes, z_scales

        def second_layer(e0, n, z_codes, z_scales, tag):
            nv = n // 2
            bank = psum_y.tile([P, BLOCKS, nv], F32, name=f"y_bank{e0}", tag="y_bank")
            for b in range(BLOCKS):
                cols = slice(P * b, P * (b + 1))
                nc.tensor.matmul_mx(
                    out=bank[:, b, :],
                    lhsT=w2_codes[:, cols].bitcast(FP8X4),
                    lhsT_scale=w2_scales[:, cols],
                    rhs=z_codes[:].bitcast(FP8X4),
                    rhs_scale=z_scales[:],
                    start=True,
                    stop=True,
                )
            y_sb[e0] = keep.tile([P, BLOCKS, nv], F32, name=f"y{e0}", tag=tag, align_bytes=64)
            nc.scalar.activation(y_sb[e0][:], bank[:], ACT.Copy)

        def scatter(b, e0, n):
            v0, nv = e0 // 2, n // 2
            cols = slice(v0, v0 + nv)
            places = pos_t[:, v0 // 16 : (v0 + nv) // 16]
            nc.vector.tensor_tensor(frames[b][:].indirect(places), y_sb[e0][:, b, :], gate_sb[:, b, cols], ALU.mult)

        hs = [first_layer(*STRETCHES[0]), first_layer(*STRETCHES[1])]
        second_layer(*STRETCHES[0], *pool_and_quantise(*STRETCHES[0], hs[0]), "y0")
        gather_words(1, 768, 256, "z0", ENTRIES)
        hs.append(first_layer(*STRETCHES[2]))
        z1 = pool_and_quantise(*STRETCHES[1], hs[1])
        z2 = pool_and_quantise(*STRETCHES[2], hs[2])
        second_layer(*STRETCHES[1], *z1, "h512")
        second_layer(*STRETCHES[2], *z2, "y2")
        for stretch in STRETCHES:
            for b in range(BLOCKS):
                scatter(b, *stretch)
                if stretch == STRETCHES[-1]:
                    nc.sync.dma_start(out=out[P * b : P * (b + 1), :], in_=frames[b][:])
